import numpy as np
import ml_dtypes


def mxq(x, axis, fmt="e4m3"):
    dtype, down = {"e4m3": (ml_dtypes.float8_e4m3fn, 7), "e5m2": (ml_dtypes.float8_e5m2, 14)}[fmt]
    v = np.moveaxis(np.asarray(x, np.float32).astype(ml_dtypes.bfloat16).astype(np.float64), axis, -1)
    blocks = v.reshape(v.shape[:-1] + (-1, 32))
    amax = np.abs(blocks).max(-1, keepdims=True)
    byte = np.maximum(np.where(amax > 0, np.frexp(amax)[1] - 1 + 127, 0) - down, 1)
    scale = np.exp2(byte - 127.0)
    codes = (blocks / scale).astype(np.float32).astype(dtype).astype(np.float64)
    return np.moveaxis((codes * scale).reshape(v.shape), -1, axis)


WIDE = False


def mx_kscale(k):
    if not WIDE:
        return np.ones(k)
    levels = np.array([10, -10, 5, -5, 0])
    if k % 512:
        return np.exp2(np.random.permutation(np.resize(levels, k // 32))).repeat(32)
    a = np.empty((k // 512, 16))
    for p in range(k // 512):
        a[p, :8] = np.random.permutation(np.resize(levels, 8))
        for g in range(8):
            far = levels[np.abs(levels - a[p, g]) >= 10]
            a[p, g + 8] = far[np.random.randint(len(far))]
    return np.exp2(a.ravel()).repeat(32)


def f64(x):
    return np.asarray(x).astype(np.float64)


E2M1 = np.array([0.0, 0.5, 1.0, 1.5, 2.0, 3.0, 4.0, 6.0, -0.0, -0.5, -1.0, -1.5, -2.0, -3.0, -4.0, -6.0])


def pack_weight(w, fmt):
    k, n = w.shape
    w = f64(np.asarray(w, np.float32).astype(ml_dtypes.bfloat16)).reshape(k // 32, 32, n)
    amax = np.abs(w).max(1)
    if fmt == "e4m3":
        byte = np.frexp(amax)[1] - 1 + 127 - 7
    else:
        mant, ex = np.frexp(amax / 6.0)
        byte = np.where(mant > 0.5, ex, ex - 1) + 127
    byte = np.clip(np.where(amax > 0, byte, 1), 1, 254)
    scaled = (w * np.exp2(127.0 - byte)[:, None, :]).reshape(k, n).astype(np.float32)
    by_word = np.ascontiguousarray(scaled.reshape(k // 512, 128, 4, n).transpose(0, 1, 3, 2))
    if fmt == "e4m3":
        words = by_word.astype(ml_dtypes.float8_e4m3fn).view(np.uint8)
    else:
        c = by_word.astype(ml_dtypes.float4_e2m1fn).view(np.uint8) & 0xF
        words = (c[..., 0::2] | (c[..., 1::2] << 4)).reshape(k // 512, 128, 2 * n)
    return np.ascontiguousarray(words), np.ascontiguousarray(byte.astype(np.uint8).reshape(k // 512, 16, n))


def unpack_weight(words, scales, fmt):
    g, _, n = scales.shape
    words = np.ascontiguousarray(words).reshape(g, 128, n, -1)
    if fmt == "e4m3":
        vals = words.view(ml_dtypes.float8_e4m3fn).astype(np.float64)
    else:
        nib = np.empty((g, 128, n, 4), np.uint8)
        nib[..., 0::2] = words & 0xF
        nib[..., 1::2] = words >> 4
        vals = E2M1[nib]
    vals = vals * np.repeat(np.exp2(scales.astype(np.float64) - 127.0), 8, axis=1)[..., None]
    return vals.transpose(0, 1, 3, 2).reshape(g * 512, n)


K, L, T, N = 1024, 1024, 512, 512


def setup_inputs():
    n = np.random.standard_normal
    fk = mx_kscale(K)
    fl = mx_kscale(L)
    xtp = pack_weight(n((K, T)) / fk[:, None], "e4m3")
    xqp = pack_weight(n((L, T)) / fl[:, None], "e2m1")
    wqp = pack_weight(n((L, N)) * 1 / np.sqrt(L) * fl[:, None], "e4m3")
    return {
        "xt_words": xtp[0],
        "xt_scales": xtp[1],
        "ea": (n((K, N)) * 1 / np.sqrt(K) * fk[:, None]).astype(np.float32),
        "eb": (n((K, N)) * 1 / np.sqrt(K) * fk[:, None]).astype(np.float32),
        "sh": (np.random.uniform(0.2, 0.8, (1, N))).astype(np.float32),
        "xq_words": xqp[0],
        "xq_scales": xqp[1],
        "wq_words": wqp[0],
        "wq_scales": wqp[1],
    }


def reference(xt_words, xt_scales, ea, eb, sh, xq_words, xq_scales, wq_words, wq_scales):
    xtu = unpack_weight(xt_words, xt_scales, "e4m3")
    xqu = unpack_weight(xq_words, xq_scales, "e2m1")
    wqu = unpack_weight(wq_words, wq_scales, "e4m3")
    em = f64(eb) + f64(sh) * (f64(ea) - f64(eb))
    emq = mxq(em, 0, "e4m3")
    y = emq.T @ xtu + wqu.T @ xqu
    return y

@@ -1,0 +1,226 @@
+from contextlib import ExitStack
+
+import concourse.mybir as mybir
+from concourse.masks import make_identity
+
+K, L, T, N = 1024, 1024, 512, 512
+FLOPS = 2 * N * T * (K + L)
+
+F32 = mybir.dt.float32
+BF16 = mybir.dt.bfloat16
+I32 = mybir.dt.int32
+U32 = mybir.dt.uint32
+U8 = mybir.dt.uint8
+FP8X4 = mybir.dt.float8_e4m3fn_x4
+FP4X4 = mybir.dt.float4_e2m1fn_x4
+COPY = mybir.ActivationFunctionType.Copy
+MULT = mybir.AluOpType.mult
+ADD = mybir.AluOpType.add
+
+P = 128
+PASSES = 2
+BLOCKS = N // P
+
+
+def tile_mix_blended_weights_and_given_kernel(
+    tc, xt_words, xt_scales, ea, eb, sh, xq_words, xq_scales, wq_words, wq_scales, out
+):
+    nc = tc.nc
+    with ExitStack() as ctx:
+        keep = ctx.enter_context(tc.tile_pool(name="keep", bufs=1))
+        sums = ctx.enter_context(tc.psum_pool(name="sums", bufs=1))
+        work = ctx.enter_context(tc.psum_pool(name="work", bufs=4))
+        ctx.enter_context(tc.manual_schedule())
+
+        ident = keep.tile([P, P], F32, name="ident")
+        make_identity(nc, ident[:])
+
+        planes = {}
+        for name in ("wq", "xq", "xt"):
+            planes[name] = keep.tile([P, PASSES, 512], U8, name=name + "_plane", align_bytes=64)
+            nc.vector.memset(planes[name][:].rearrange("p g n -> p (g n)").bitcast(I32), 0)
+
+        def load_scales(queue, name, scales):
+            for q in range(4):
+                queue.dma_start(
+                    out=planes[name][32 * q : 32 * q + 4, :, :].bitcast(I32),
+                    in_=scales[:, 4 * q : 4 * q + 4, :].rearrange("g r n -> r g n").bitcast(I32),
+                )
+
+        raw = {}
+
+        def load_rows(name, src, g, u):
+            raw[name, g, u] = keep.tile([P, 2, N], F32, name="%s_%d_%d" % (name, g, u))
+            rows = src[512 * g : 512 * (g + 1), :].rearrange("(p j) n -> p j n", j=4)
+            nc.sync.dma_start(out=raw[name, g, u][:], in_=rows[:, 2 * u : 2 * u + 2, :])
+
+        codes = {}
+
+        def load_fp8(name, words, g):
+            codes[name, g] = keep.tile([P, 512], U32, name="%s_codes_%d" % (name, g), align_bytes=64)
+            nc.sync.dma_start(
+                out=codes[name, g][:].bitcast(I32),
+                in_=words[g].rearrange("p n t -> p (n t)").bitcast(I32),
+            )
+
+        def load_fp4(g):
+            codes["xq", g] = keep.tile([P, 2 * T], U8, name="xq_codes_%d" % g, align_bytes=64)
+            nc.sync.dma_start(out=codes["xq", g][:].bitcast(I32), in_=xq_words[g].bitcast(I32))
+
+        share = keep.tile([P, BLOCKS], F32, name="share")
+        rest = keep.tile([P, BLOCKS], F32, name="rest")
+
+        with nc.allow_non_contiguous_dma(reason="one share for each partition and block"):
+            nc.scalar.dma_start(out=share[:], in_=sh.rearrange("o (b p) -> p (o b)", p=P))
+        load_rows("ea", ea, 0, 0)
+        load_rows("eb", eb, 0, 0)
+        load_rows("ea", ea, 0, 1)
+        load_scales(nc.sync, "wq", wq_scales)
+        load_rows("eb", eb, 0, 1)
+        load_fp4(0)
+        load_fp8("wq", wq_words, 0)
+        load_scales(nc.sync, "xq", xq_scales)
+        load_rows("ea", ea, 1, 0)
+        load_scales(nc.sync, "xt", xt_scales)
+        load_rows("eb", eb, 1, 0)
+        load_fp8("xt", xt_words, 0)
+        load_rows("ea", ea, 1, 1)
+        load_rows("eb", eb, 1, 1)
+        load_fp4(1)
+        load_fp8("wq", wq_words, 1)
+        load_fp8("xt", xt_words, 1)
+
+        nc.scalar.activation(out=rest[:], in_=share[:], func=COPY, scale=-1.0, bias=1.0)
+
+        acc = [sums.tile([P, T], F32, name="acc_%d" % b) for b in range(BLOCKS)]
+        part = {}
+        blend = {}
+        grouped = {}
+        em_codes = {}
+        em_plane = {}
+        for g in range(PASSES):
+            grouped[g] = keep.tile([P, N * 4], BF16, name="grouped_%d" % g, align_bytes=64)
+            em_codes[g] = keep.tile([P, N], U32, name="em_codes_%d" % g, align_bytes=64)
+            em_plane[g] = keep.tile([P, N], U8, name="em_plane_%d" % g, align_bytes=64)
+
+        def turn(name, g, u, pair):
+            bank = work.tile([P, 2, 2, P], F32, name="bank")
+            for i in range(2):
+                b = 2 * pair + i
+                for e in range(2):
+                    nc.tensor.transpose(
+                        bank[:, i, e, :], raw[name, g, u][:, e, P * b : P * (b + 1)], ident[:]
+                    )
+            return bank
+
+        def first_matrix(g, u):
+            for pair in range(2):
+                bank = turn("ea", g, u, pair)
+                for i in range(2):
+                    b = 2 * pair + i
+                    part[g, u, b] = keep.tile([P, P, 2], F32, name="part_%d_%d_%d" % (g, u, b))
+                    nc.scalar.activation(
+                        out=part[g, u, b][:],
+                        in_=bank[:, i, :, :].rearrange("n e p -> n p e"),
+                        func=COPY,
+                        scale=share[:, b : b + 1],
+                    )
+
+        def second_matrix(g, u):
+            for pair in range(2):
+                bank = turn("eb", g, u, pair)
+                for i in range(2):
+                    b = 2 * pair + i
+                    blend[g, u, b] = keep.tile([P, P, 2], BF16, name="blend_%d_%d_%d" % (g, u, b))
+                    nc.vector.scalar_tensor_tensor(
+                        out=blend[g, u, b][:],
+                        in0=bank[:, i, :, :].rearrange("n e p -> n p e"),
+                        scalar=rest[:, b : b + 1],
+                        in1=part[g, u, b][:],
+                        op0=MULT,
+                        op1=ADD,
+                    )
+
+        def turn_back(g, pair, split):
+            bank = work.tile([P, 2, 2, P], F32, name="bank")
+            for i in range(2):
+                for u in range(2):
+                    words = blend[g, u, 2 * pair + i][:].rearrange("n p e -> n (p e)").bitcast(F32)
+                    nc.tensor.transpose(bank[:, i, u, :], words, ident[:])
+            dst = grouped[g][:].bitcast(F32).rearrange("p (b n u) -> p b n u", b=BLOCKS, u=2)
+            src = bank[:].rearrange("p i u n -> p i n u")
+            if split:
+                for i in range(2):
+                    nc.scalar.copy(out=dst[:, 2 * pair + i, :, :], in_=src[:, i, :, :])
+            else:
+                nc.scalar.copy(out=dst[:, 2 * pair : 2 * pair + 2, :, :], in_=src)
+
+        def quantise(g, b0, b1):
+            nc.vector.quantize_mx(
+                out=em_codes[g][:, P * b0 : P * b1].bitcast(FP8X4),
+                scales=em_plane[g][:, P * b0 : P * b1],
+                in_=grouped[g][:, 4 * P * b0 : 4 * P * b1],
+            )
+
+        def given_pass(g, b):
+            cols = slice(P * b, P * (b + 1))
+            nc.tensor.matmul_mx(
+                out=acc[b][:],
+                lhsT=codes["wq", g][:, cols].bitcast(FP8X4),
+                lhsT_scale=planes["wq"][:, g, cols],
+                rhs=codes["xq", g][:].bitcast(FP4X4),
+                rhs_scale=planes["xq"][:, g, :],
+                start=(g == 0),
+                stop=False,
+            )
+
+        def blended_pass(g, b):
+            cols = slice(P * b, P * (b + 1))
+            nc.tensor.matmul_mx(
+                out=acc[b][:],
+                lhsT=em_codes[g][:, cols].bitcast(FP8X4),
+                lhsT_scale=em_plane[g][:, cols],
+                rhs=codes["xt", g][:].bitcast(FP8X4),
+                rhs_scale=planes["xt"][:, g, :],
+                start=False,
+                stop=(g == PASSES - 1),
+            )
+
+        def finish(b):
+            result = keep.tile([P, T], F32, name="result_%d" % b)
+            if b % 2 == 0:
+                nc.scalar.copy(out=result[:], in_=acc[b][:])
+            else:
+                nc.vector.tensor_copy(out=result[:], in_=acc[b][:])
+            nc.sync.dma_start(out=out[P * b : P * (b + 1), :], in_=result[:])
+
+        first_matrix(0, 0)
+        second_matrix(0, 0)
+        first_matrix(0, 1)
+        second_matrix(0, 1)
+        for b in range(BLOCKS):
+            given_pass(0, b)
+        for pair in range(2):
+            turn_back(0, pair, False)
+        first_matrix(1, 0)
+        for pair in range(2):
+            quantise(0, 2 * pair, 2 * pair + 2)
+        second_matrix(1, 0)
+        for b in range(BLOCKS):
+            blended_pass(0, b)
+        first_matrix(1, 1)
+        second_matrix(1, 1)
+        turn_back(1, 0, True)
+        given_pass(1, 0)
+        given_pass(1, 1)
+        turn_back(1, 1, True)
+        for b in range(BLOCKS):
+            quantise(1, b, b + 1)
+        blended_pass(1, 0)
+        blended_pass(1, 1)
+        given_pass(1, 2)
+        given_pass(1, 3)
+        blended_pass(1, 2)
+        blended_pass(1, 3)
+        for b in range(BLOCKS):
+            finish(b)

@@ -29,14 +29,13 @@ def tile_mix_blended_weights_and_given_kernel(
     with ExitStack() as ctx:
         keep = ctx.enter_context(tc.tile_pool(name="keep", bufs=1))
         sums = ctx.enter_context(tc.psum_pool(name="sums", bufs=1))
-        work = ctx.enter_context(tc.psum_pool(name="work", bufs=4))
         ctx.enter_context(tc.manual_schedule())
 
         ident = keep.tile([P, P], F32, name="ident")
         make_identity(nc, ident[:])
 
         planes = {}
-        for name in ("wq", "xq", "xt"):
+        for name in ("xt", "wq", "xq"):
             planes[name] = keep.tile([P, PASSES, 512], U8, name=name + "_plane", align_bytes=64)
             nc.vector.memset(planes[name][:].rearrange("p g n -> p (g n)").bitcast(I32), 0)
 
@@ -47,180 +46,184 @@ def tile_mix_blended_weights_and_given_kernel(
                     in_=scales[:, 4 * q : 4 * q + 4, :].rearrange("g r n -> r g n").bitcast(I32),
                 )
 
+        source = {"ea": ea, "eb": eb}
         raw = {}
 
-        def load_rows(name, src, g, u):
-            raw[name, g, u] = keep.tile([P, 2, N], F32, name="%s_%d_%d" % (name, g, u))
-            rows = src[512 * g : 512 * (g + 1), :].rearrange("(p j) n -> p j n", j=4)
-            nc.sync.dma_start(out=raw[name, g, u][:], in_=rows[:, 2 * u : 2 * u + 2, :])
+        def load_rows(name, g, u0, u1, b0, b1):
+            tile = keep.tile(
+                [P, 2 * (u1 - u0), P * (b1 - b0)], F32, name="%s_%d_%d_%d" % (name, g, u0, b0)
+            )
+            rows = source[name][512 * g : 512 * (g + 1), P * b0 : P * b1].rearrange("(p j) n -> p j n", j=4)
+            nc.sync.dma_start(out=tile[:], in_=rows[:, 2 * u0 : 2 * u1, :])
+            raw[name, g, u0, b0] = tile
 
         codes = {}
 
-        def load_fp8(name, words, g):
-            codes[name, g] = keep.tile([P, 512], U32, name="%s_codes_%d" % (name, g), align_bytes=64)
+        def load_fp8(name, words):
+            codes[name] = keep.tile([P, PASSES, 512], U32, name=name + "_codes", align_bytes=64)
             nc.sync.dma_start(
-                out=codes[name, g][:].bitcast(I32),
-                in_=words[g].rearrange("p n t -> p (n t)").bitcast(I32),
+                out=codes[name][:].bitcast(I32),
+                in_=words.rearrange("g p n t -> p g (n t)").bitcast(I32),
             )
 
-        def load_fp4(g):
-            codes["xq", g] = keep.tile([P, 2 * T], U8, name="xq_codes_%d" % g, align_bytes=64)
-            nc.sync.dma_start(out=codes["xq", g][:].bitcast(I32), in_=xq_words[g].bitcast(I32))
+        def load_fp4():
+            codes["xq"] = keep.tile([P, PASSES, 2 * T], U8, name="xq_codes", align_bytes=64)
+            nc.sync.dma_start(
+                out=codes["xq"][:].bitcast(I32), in_=xq_words.rearrange("g p c -> p g c").bitcast(I32)
+            )
 
         share = keep.tile([P, BLOCKS], F32, name="share")
         rest = keep.tile([P, BLOCKS], F32, name="rest")
 
-        with nc.allow_non_contiguous_dma(reason="one share for each partition and block"):
-            nc.scalar.dma_start(out=share[:], in_=sh.rearrange("o (b p) -> p (o b)", p=P))
-        load_rows("ea", ea, 0, 0)
-        load_rows("eb", eb, 0, 0)
-        load_rows("ea", ea, 0, 1)
+        nc.scalar.dma_start(out=share[:], in_=sh.rearrange("o (p c) -> p (o c)", p=P))
+        load_scales(nc.gpsimd, "xt", xt_scales)
+        load_rows("ea", 0, 0, 1, 0, 4)
+        load_rows("eb", 0, 0, 1, 0, 4)
+        load_rows("ea", 0, 1, 2, 0, 4)
         load_scales(nc.sync, "wq", wq_scales)
-        load_rows("eb", eb, 0, 1)
-        load_fp4(0)
-        load_fp8("wq", wq_words, 0)
+        load_rows("eb", 0, 1, 2, 0, 4)
+        load_fp4()
+        load_fp8("wq", wq_words)
+        load_rows("ea", 1, 0, 2, 0, 2)
         load_scales(nc.sync, "xq", xq_scales)
-        load_rows("ea", ea, 1, 0)
-        load_scales(nc.sync, "xt", xt_scales)
-        load_rows("eb", eb, 1, 0)
-        load_fp8("xt", xt_words, 0)
-        load_rows("ea", ea, 1, 1)
-        load_rows("eb", eb, 1, 1)
-        load_fp4(1)
-        load_fp8("wq", wq_words, 1)
-        load_fp8("xt", xt_words, 1)
+        load_rows("eb", 1, 0, 2, 0, 2)
+        load_fp8("xt", xt_words)
+        for b in (2, 3):
+            load_rows("ea", 1, 0, 2, b, b + 1)
+            load_rows("eb", 1, 0, 2, b, b + 1)
 
         nc.scalar.activation(out=rest[:], in_=share[:], func=COPY, scale=-1.0, bias=1.0)
 
         acc = [sums.tile([P, T], F32, name="acc_%d" % b) for b in range(BLOCKS)]
+        spread = {}
+        for name, column in (("ea", share), ("eb", rest)):
+            spread[name] = sums.tile([P, N], F32, name="spread_" + name)
+            for c in range(4):
+                nc.tensor.transpose(
+                    spread[name][:, c : N : 4], column[:, c : c + 1].to_broadcast([P, P]), ident[:]
+                )
+
         part = {}
-        blend = {}
+        pairs = {}
         grouped = {}
         em_codes = {}
         em_plane = {}
+        for g, b0, b1 in ((0, 0, 2), (0, 2, 4), (1, 0, 1), (1, 1, 2), (1, 2, 3), (1, 3, 4)):
+            width = 4 * P * (b1 - b0)
+            grouped[g, b0] = keep.tile([P, width], BF16, name="grouped_%d_%d" % (g, b0), align_bytes=64)
+            pairs[g, b0] = keep.tile([P, width], BF16, name="pairs_%d_%d" % (g, b0))
+            for name in ("ea", "eb"):
+                part[name, g, b0] = keep.tile([P, width], F32, name="part_%s_%d_%d" % (name, g, b0))
         for g in range(PASSES):
-            grouped[g] = keep.tile([P, N * 4], BF16, name="grouped_%d" % g, align_bytes=64)
             em_codes[g] = keep.tile([P, N], U32, name="em_codes_%d" % g, align_bytes=64)
             em_plane[g] = keep.tile([P, N], U8, name="em_plane_%d" % g, align_bytes=64)
 
-        def turn(name, g, u, pair):
-            bank = work.tile([P, 2, 2, P], F32, name="bank")
-            for i in range(2):
-                b = 2 * pair + i
-                for e in range(2):
-                    nc.tensor.transpose(
-                        bank[:, i, e, :], raw[name, g, u][:, e, P * b : P * (b + 1)], ident[:]
-                    )
-            return bank
+        def weigh(name, g, b0, b1, u0, u1, first):
+            us = u1 - u0
+            n = P * (b1 - b0)
+            src = raw[name, g, u0, first][:, :, P * (b0 - first) : P * (b1 - first)]
+            factor = spread[name][:, P * b0 : P * b1].unsqueeze(1).unsqueeze(3).to_broadcast([P, us, n, 2])
+            nc.vector.tensor_tensor(
+                out=part[name, g, b0][:, 2 * n * u0 : 2 * n * u1].rearrange("p (u n e) -> p u n e", u=us, e=2),
+                in0=src.rearrange("p (u e) n -> p u n e", e=2),
+                in1=factor,
+                op=MULT,
+            )
 
-        def first_matrix(g, u):
-            for pair in range(2):
-                bank = turn("ea", g, u, pair)
-                for i in range(2):
-                    b = 2 * pair + i
-                    part[g, u, b] = keep.tile([P, P, 2], F32, name="part_%d_%d_%d" % (g, u, b))
-                    nc.scalar.activation(
-                        out=part[g, u, b][:],
-                        in_=bank[:, i, :, :].rearrange("n e p -> n p e"),
-                        func=COPY,
-                        scale=share[:, b : b + 1],
-                    )
+        def add_aside(g, b0, b1, u0, u1):
+            n = P * (b1 - b0)
+            cols = slice(2 * n * u0, 2 * n * u1)
+            nc.gpsimd.tensor_tensor(
+                out=pairs[g, b0][:, cols], in0=part["ea", g, b0][:, cols], in1=part["eb", g, b0][:, cols], op=ADD
+            )
 
-        def second_matrix(g, u):
-            for pair in range(2):
-                bank = turn("eb", g, u, pair)
-                for i in range(2):
-                    b = 2 * pair + i
-                    blend[g, u, b] = keep.tile([P, P, 2], BF16, name="blend_%d_%d_%d" % (g, u, b))
-                    nc.vector.scalar_tensor_tensor(
-                        out=blend[g, u, b][:],
-                        in0=bank[:, i, :, :].rearrange("n e p -> n p e"),
-                        scalar=rest[:, b : b + 1],
-                        in1=part[g, u, b][:],
-                        op0=MULT,
-                        op1=ADD,
-                    )
+        def weave(g, b0):
+            words = pairs[g, b0][:].bitcast(F32).rearrange("p (u n) -> p n u", u=2)
+            nc.scalar.copy(out=grouped[g, b0][:].bitcast(F32).rearrange("p (n u) -> p n u", u=2), in_=words)
 
-        def turn_back(g, pair, split):
-            bank = work.tile([P, 2, 2, P], F32, name="bank")
-            for i in range(2):
-                for u in range(2):
-                    words = blend[g, u, 2 * pair + i][:].rearrange("n p e -> n (p e)").bitcast(F32)
-                    nc.tensor.transpose(bank[:, i, u, :], words, ident[:])
-            dst = grouped[g][:].bitcast(F32).rearrange("p (b n u) -> p b n u", b=BLOCKS, u=2)
-            src = bank[:].rearrange("p i u n -> p i n u")
-            if split:
-                for i in range(2):
-                    nc.scalar.copy(out=dst[:, 2 * pair + i, :, :], in_=src[:, i, :, :])
-            else:
-                nc.scalar.copy(out=dst[:, 2 * pair : 2 * pair + 2, :, :], in_=src)
+        def add_here(g, b):
+            nc.vector.tensor_tensor(
+                out=grouped[g, b][:].rearrange("p (n u e) -> p n u e", u=2, e=2),
+                in0=part["ea", g, b][:].rearrange("p (u n e) -> p n u e", u=2, e=2),
+                in1=part["eb", g, b][:].rearrange("p (u n e) -> p n u e", u=2, e=2),
+                op=ADD,
+            )
 
         def quantise(g, b0, b1):
             nc.vector.quantize_mx(
                 out=em_codes[g][:, P * b0 : P * b1].bitcast(FP8X4),
                 scales=em_plane[g][:, P * b0 : P * b1],
-                in_=grouped[g][:, 4 * P * b0 : 4 * P * b1],
+                in_=grouped[g, b0][:],
             )
 
-        def given_pass(g, b):
+        def given_pass(g, b, start=False, stop=False):
             cols = slice(P * b, P * (b + 1))
             nc.tensor.matmul_mx(
                 out=acc[b][:],
-                lhsT=codes["wq", g][:, cols].bitcast(FP8X4),
+                lhsT=codes["wq"][:, g, cols].bitcast(FP8X4),
                 lhsT_scale=planes["wq"][:, g, cols],
-                rhs=codes["xq", g][:].bitcast(FP4X4),
+                rhs=codes["xq"][:, g, :].bitcast(FP4X4),
                 rhs_scale=planes["xq"][:, g, :],
-                start=(g == 0),
-                stop=False,
+                start=start,
+                stop=stop,
             )
 
-        def blended_pass(g, b):
+        def blended_pass(g, b, start=False, stop=False):
             cols = slice(P * b, P * (b + 1))
             nc.tensor.matmul_mx(
                 out=acc[b][:],
                 lhsT=em_codes[g][:, cols].bitcast(FP8X4),
                 lhsT_scale=em_plane[g][:, cols],
-                rhs=codes["xt", g][:].bitcast(FP8X4),
+                rhs=codes["xt"][:, g, :].bitcast(FP8X4),
                 rhs_scale=planes["xt"][:, g, :],
-                start=False,
-                stop=(g == PASSES - 1),
+                start=start,
+                stop=stop,
             )
 
         def finish(b):
             result = keep.tile([P, T], F32, name="result_%d" % b)
-            if b % 2 == 0:
-                nc.scalar.copy(out=result[:], in_=acc[b][:])
-            else:
-                nc.vector.tensor_copy(out=result[:], in_=acc[b][:])
+            nc.scalar.copy(out=result[:], in_=acc[b][:])
             nc.sync.dma_start(out=out[P * b : P * (b + 1), :], in_=result[:])
 
-        first_matrix(0, 0)
-        second_matrix(0, 0)
-        first_matrix(0, 1)
-        second_matrix(0, 1)
-        for b in range(BLOCKS):
-            given_pass(0, b)
-        for pair in range(2):
-            turn_back(0, pair, False)
-        first_matrix(1, 0)
-        for pair in range(2):
-            quantise(0, 2 * pair, 2 * pair + 2)
-        second_matrix(1, 0)
+        for u in range(2):
+            for b in (0, 2):
+                weigh("ea", 0, b, b + 2, u, u + 1, 0)
+            for b in (0, 2):
+                weigh("eb", 0, b, b + 2, u, u + 1, 0)
+                add_aside(0, b, b + 2, u, u + 1)
+        for b in (0, 2):
+            weave(0, b)
+        for g in range(PASSES):
+            for b in range(BLOCKS):
+                given_pass(g, b, start=(g == 0))
+        weigh("ea", 1, 0, 1, 0, 2, 0)
+        weigh("ea", 1, 1, 2, 0, 2, 0)
+        quantise(0, 0, 2)
+        weigh("eb", 1, 0, 1, 0, 2, 0)
+        add_aside(1, 0, 1, 0, 2)
+        weave(1, 0)
+        quantise(0, 2, 4)
+        weigh("eb", 1, 1, 2, 0, 2, 0)
+        add_aside(1, 1, 2, 0, 2)
+        weave(1, 1)
         for b in range(BLOCKS):
             blended_pass(0, b)
-        first_matrix(1, 1)
-        second_matrix(1, 1)
-        turn_back(1, 0, True)
-        given_pass(1, 0)
-        given_pass(1, 1)
-        turn_back(1, 1, True)
-        for b in range(BLOCKS):
-            quantise(1, b, b + 1)
-        blended_pass(1, 0)
-        blended_pass(1, 1)
-        given_pass(1, 2)
-        given_pass(1, 3)
-        blended_pass(1, 2)
-        blended_pass(1, 3)
-        for b in range(BLOCKS):
-            finish(b)
+        weigh("ea", 1, 2, 3, 0, 2, 2)
+        weigh("eb", 1, 2, 3, 0, 2, 2)
+        add_aside(1, 2, 3, 0, 2)
+        quantise(1, 0, 1)
+        blended_pass(1, 0, stop=True)
+        weigh("ea", 1, 3, 4, 0, 2, 3)
+        quantise(1, 1, 2)
+        blended_pass(1, 1, stop=True)
+        weave(1, 2)
+        finish(0)
+        weigh("eb", 1, 3, 4, 0, 2, 3)
+        add_here(1, 3)
+        quantise(1, 2, 3)
+        blended_pass(1, 2, stop=True)
+        finish(1)
+        quantise(1, 3, 4)
+        blended_pass(1, 3, stop=True)
+        finish(2)
+        finish(3)

@@ -13,13 +13,14 @@ U32 = mybir.dt.uint32
 U8 = mybir.dt.uint8
 FP8X4 = mybir.dt.float8_e4m3fn_x4
 FP4X4 = mybir.dt.float4_e2m1fn_x4
-COPY = mybir.ActivationFunctionType.Copy
 MULT = mybir.AluOpType.mult
-ADD = mybir.AluOpType.add
+SUBTRACT = mybir.AluOpType.subtract
 
 P = 128
+PACK = 4
 PASSES = 2
 BLOCKS = N // P
+WIDTH = PACK * P
 
 
 def tile_mix_blended_weights_and_given_kernel(
@@ -35,195 +36,184 @@ def tile_mix_blended_weights_and_given_kernel(
         make_identity(nc, ident[:])
 
         planes = {}
-        for name in ("xt", "wq", "xq"):
+        for name in ("wq", "xq"):
             planes[name] = keep.tile([P, PASSES, 512], U8, name=name + "_plane", align_bytes=64)
             nc.vector.memset(planes[name][:].rearrange("p g n -> p (g n)").bitcast(I32), 0)
+        xt_plane = keep.tile([P, T], U8, name="xt_plane", align_bytes=64)
+        nc.vector.memset(xt_plane[:].bitcast(I32), 0)
 
-        def load_scales(queue, name, scales):
+        def load_scales(name, scales):
+            rows = scales.rearrange("g (q r) n -> r q g n", r=4)
+            for r in range(4):
+                nc.sync.dma_start(out=planes[name][r:P:32, :, :].bitcast(I32), in_=rows[r].bitcast(I32))
+
+        def load_xt_scales():
             for q in range(4):
-                queue.dma_start(
-                    out=planes[name][32 * q : 32 * q + 4, :, :].bitcast(I32),
-                    in_=scales[:, 4 * q : 4 * q + 4, :].rearrange("g r n -> r g n").bitcast(I32),
+                nc.sync.dma_start(
+                    out=xt_plane[32 * q + 4 : 32 * q + 12, :].bitcast(I32),
+                    in_=xt_scales[:, 4 * q : 4 * q + 4, :].bitcast(I32),
                 )
 
         source = {"ea": ea, "eb": eb}
         raw = {}
 
-        def load_rows(name, g, u0, u1, b0, b1):
-            tile = keep.tile(
-                [P, 2 * (u1 - u0), P * (b1 - b0)], F32, name="%s_%d_%d_%d" % (name, g, u0, b0)
-            )
-            rows = source[name][512 * g : 512 * (g + 1), P * b0 : P * b1].rearrange("(p j) n -> p j n", j=4)
-            nc.sync.dma_start(out=tile[:], in_=rows[:, 2 * u0 : 2 * u1, :])
-            raw[name, g, u0, b0] = tile
+        def load_rows(name, g, b0, b1):
+            tile = keep.tile([P, PACK, P * (b1 - b0)], F32, name="%s_%d_%d" % (name, g, b0))
+            rows = source[name][512 * g : 512 * (g + 1), P * b0 : P * b1]
+            nc.sync.dma_start(out=tile[:], in_=rows.rearrange("(p j) n -> p j n", j=PACK))
+            for b in range(b0, b1):
+                raw[name, g, b] = tile[:, :, P * (b - b0) : P * (b - b0 + 1)]
 
         codes = {}
 
-        def load_fp8(name, words):
-            codes[name] = keep.tile([P, PASSES, 512], U32, name=name + "_codes", align_bytes=64)
+        def load_fp8(name, words, g):
+            codes[name, g] = keep.tile([P, 512], U32, name="%s_codes_%d" % (name, g), align_bytes=64)
             nc.sync.dma_start(
-                out=codes[name][:].bitcast(I32),
-                in_=words.rearrange("g p n t -> p g (n t)").bitcast(I32),
+                out=codes[name, g][:].bitcast(I32),
+                in_=words[g].rearrange("p n t -> p (n t)").bitcast(I32),
             )
 
-        def load_fp4():
-            codes["xq"] = keep.tile([P, PASSES, 2 * T], U8, name="xq_codes", align_bytes=64)
-            nc.sync.dma_start(
-                out=codes["xq"][:].bitcast(I32), in_=xq_words.rearrange("g p c -> p g c").bitcast(I32)
-            )
+        def load_fp4(g):
+            codes["xq", g] = keep.tile([P, 2 * T], U8, name="xq_codes_%d" % g, align_bytes=64)
+            nc.sync.dma_start(out=codes["xq", g][:].bitcast(I32), in_=xq_words[g].bitcast(I32))
 
-        share = keep.tile([P, BLOCKS], F32, name="share")
-        rest = keep.tile([P, BLOCKS], F32, name="rest")
-
+        share = keep.tile([P, PACK], F32, name="share")
         nc.scalar.dma_start(out=share[:], in_=sh.rearrange("o (p c) -> p (o c)", p=P))
-        load_scales(nc.gpsimd, "xt", xt_scales)
-        load_rows("ea", 0, 0, 1, 0, 4)
-        load_rows("eb", 0, 0, 1, 0, 4)
-        load_rows("ea", 0, 1, 2, 0, 4)
-        load_scales(nc.sync, "wq", wq_scales)
-        load_rows("eb", 0, 1, 2, 0, 4)
-        load_fp4()
-        load_fp8("wq", wq_words)
-        load_rows("ea", 1, 0, 2, 0, 2)
-        load_scales(nc.sync, "xq", xq_scales)
-        load_rows("eb", 1, 0, 2, 0, 2)
-        load_fp8("xt", xt_words)
-        for b in (2, 3):
-            load_rows("ea", 1, 0, 2, b, b + 1)
-            load_rows("eb", 1, 0, 2, b, b + 1)
-
-        nc.scalar.activation(out=rest[:], in_=share[:], func=COPY, scale=-1.0, bias=1.0)
+        for b in range(2):
+            load_rows("ea", 0, b, b + 1)
+            load_rows("eb", 0, b, b + 1)
+        load_rows("ea", 0, 2, 4)
+        load_scales("wq", wq_scales)
+        load_rows("eb", 0, 2, 4)
+        load_scales("xq", xq_scales)
+        load_fp4(0)
+        load_rows("ea", 1, 0, 2)
+        load_rows("eb", 1, 0, 2)
+        load_fp8("wq", wq_words, 0)
+        load_xt_scales()
+        load_fp8("xt", xt_words, 0)
+        load_fp4(1)
+        load_rows("ea", 1, 2, 3)
+        load_rows("eb", 1, 2, 3)
+        load_fp8("wq", wq_words, 1)
+        load_rows("ea", 1, 3, 4)
+        load_rows("eb", 1, 3, 4)
+        load_fp8("xt", xt_words, 1)
 
         acc = [sums.tile([P, T], F32, name="acc_%d" % b) for b in range(BLOCKS)]
-        spread = {}
-        for name, column in (("ea", share), ("eb", rest)):
-            spread[name] = sums.tile([P, N], F32, name="spread_" + name)
-            for c in range(4):
-                nc.tensor.transpose(
-                    spread[name][:, c : N : 4], column[:, c : c + 1].to_broadcast([P, P]), ident[:]
-                )
+        spread = sums.tile([P, N], F32, name="spread")
+        for c in range(PACK):
+            nc.tensor.transpose(spread[:, c:N:PACK], share[:, c : c + 1].to_broadcast([P, P]), ident[:])
 
-        part = {}
-        pairs = {}
+        tiles = [(g, b) for g in range(PASSES) for b in range(BLOCKS)]
+        first = {}
+        second = {}
+        total = {}
         grouped = {}
-        em_codes = {}
-        em_plane = {}
-        for g, b0, b1 in ((0, 0, 2), (0, 2, 4), (1, 0, 1), (1, 1, 2), (1, 2, 3), (1, 3, 4)):
-            width = 4 * P * (b1 - b0)
-            grouped[g, b0] = keep.tile([P, width], BF16, name="grouped_%d_%d" % (g, b0), align_bytes=64)
-            pairs[g, b0] = keep.tile([P, width], BF16, name="pairs_%d_%d" % (g, b0))
-            for name in ("ea", "eb"):
-                part[name, g, b0] = keep.tile([P, width], F32, name="part_%s_%d_%d" % (name, g, b0))
-        for g in range(PASSES):
-            em_codes[g] = keep.tile([P, N], U32, name="em_codes_%d" % g, align_bytes=64)
-            em_plane[g] = keep.tile([P, N], U8, name="em_plane_%d" % g, align_bytes=64)
+        for g, b in tiles:
+            first[g, b] = keep.tile([P, WIDTH], F32, name="first_%d_%d" % (g, b))
+            second[g, b] = keep.tile([P, WIDTH], F32, name="second_%d_%d" % (g, b))
+            total[g, b] = keep.tile([P, WIDTH], BF16, name="total_%d_%d" % (g, b))
+            grouped[g, b] = keep.tile([P, WIDTH], BF16, name="grouped_%d_%d" % (g, b), align_bytes=64)
+        em_codes = [keep.tile([P, N], U32, name="em_codes_%d" % g, align_bytes=64) for g in range(PASSES)]
+        em_plane = [keep.tile([P, N], U8, name="em_plane_%d" % g, align_bytes=64) for g in range(PASSES)]
 
-        def weigh(name, g, b0, b1, u0, u1, first):
-            us = u1 - u0
-            n = P * (b1 - b0)
-            src = raw[name, g, u0, first][:, :, P * (b0 - first) : P * (b1 - first)]
-            factor = spread[name][:, P * b0 : P * b1].unsqueeze(1).unsqueeze(3).to_broadcast([P, us, n, 2])
+        def factor(b, rows):
+            return spread[:, P * b : P * (b + 1)].unsqueeze(1).to_broadcast([P, rows, P])
+
+        def weigh_first(g, b):
             nc.vector.tensor_tensor(
-                out=part[name, g, b0][:, 2 * n * u0 : 2 * n * u1].rearrange("p (u n e) -> p u n e", u=us, e=2),
-                in0=src.rearrange("p (u e) n -> p u n e", e=2),
-                in1=factor,
+                out=first[g, b][:].rearrange("p (j n) -> p j n", j=PACK),
+                in0=raw["ea", g, b],
+                in1=factor(b, PACK),
                 op=MULT,
             )
 
-        def add_aside(g, b0, b1, u0, u1):
-            n = P * (b1 - b0)
-            cols = slice(2 * n * u0, 2 * n * u1)
-            nc.gpsimd.tensor_tensor(
-                out=pairs[g, b0][:, cols], in0=part["ea", g, b0][:, cols], in1=part["eb", g, b0][:, cols], op=ADD
+        def weigh_second(g, b, j0, j1):
+            nc.vector.scalar_tensor_tensor(
+                out=second[g, b][:, P * j0 : P * j1].rearrange("p (j n) -> p j n", j=j1 - j0),
+                in0=factor(b, j1 - j0),
+                scalar=1.0,
+                in1=raw["eb", g, b][:, j0:j1, :],
+                op0=SUBTRACT,
+                op1=MULT,
             )
 
-        def weave(g, b0):
-            words = pairs[g, b0][:].bitcast(F32).rearrange("p (u n) -> p n u", u=2)
-            nc.scalar.copy(out=grouped[g, b0][:].bitcast(F32).rearrange("p (n u) -> p n u", u=2), in_=words)
-
-        def add_here(g, b):
-            nc.vector.tensor_tensor(
-                out=grouped[g, b][:].rearrange("p (n u e) -> p n u e", u=2, e=2),
-                in0=part["ea", g, b][:].rearrange("p (u n e) -> p n u e", u=2, e=2),
-                in1=part["eb", g, b][:].rearrange("p (u n e) -> p n u e", u=2, e=2),
-                op=ADD,
+        def join(engine, g, b, j0, j1):
+            cols = slice(P * j0, P * j1)
+            engine.tensor_tensor(
+                out=total[g, b][:, cols], in0=first[g, b][:, cols], in1=second[g, b][:, cols], op=SUBTRACT
             )
 
-        def quantise(g, b0, b1):
+        def weave(copy, g, b):
+            copy(
+                out=grouped[g, b][:].rearrange("p (n j) -> p n j", j=PACK),
+                in_=total[g, b][:].rearrange("p (j n) -> p n j", j=PACK),
+            )
+
+        def quantise(g, b):
             nc.vector.quantize_mx(
-                out=em_codes[g][:, P * b0 : P * b1].bitcast(FP8X4),
-                scales=em_plane[g][:, P * b0 : P * b1],
-                in_=grouped[g, b0][:],
+                out=em_codes[g][:, P * b : P * (b + 1)].bitcast(FP8X4),
+                scales=em_plane[g][:, P * b : P * (b + 1)],
+                in_=grouped[g, b][:],
             )
 
-        def given_pass(g, b, start=False, stop=False):
+        def given_pass(g, b):
             cols = slice(P * b, P * (b + 1))
             nc.tensor.matmul_mx(
                 out=acc[b][:],
-                lhsT=codes["wq"][:, g, cols].bitcast(FP8X4),
+                lhsT=codes["wq", g][:, cols].bitcast(FP8X4),
                 lhsT_scale=planes["wq"][:, g, cols],
-                rhs=codes["xq"][:, g, :].bitcast(FP4X4),
+                rhs=codes["xq", g][:].bitcast(FP4X4),
                 rhs_scale=planes["xq"][:, g, :],
-                start=start,
-                stop=stop,
+                start=(g == 0),
+                stop=False,
             )
 
-        def blended_pass(g, b, start=False, stop=False):
+        def blended_pass(g, b):
             cols = slice(P * b, P * (b + 1))
             nc.tensor.matmul_mx(
                 out=acc[b][:],
                 lhsT=em_codes[g][:, cols].bitcast(FP8X4),
                 lhsT_scale=em_plane[g][:, cols],
-                rhs=codes["xt"][:, g, :].bitcast(FP8X4),
-                rhs_scale=planes["xt"][:, g, :],
-                start=start,
-                stop=stop,
+                rhs=codes["xt", g][:].bitcast(FP8X4),
+                rhs_scale=xt_plane[4 + 4 * g : P, :],
+                start=False,
+                stop=(g == PASSES - 1),
             )
 
-        def finish(b):
+        def finish(copy, b):
             result = keep.tile([P, T], F32, name="result_%d" % b)
-            nc.scalar.copy(out=result[:], in_=acc[b][:])
+            copy(out=result[:], in_=acc[b][:])
             nc.sync.dma_start(out=out[P * b : P * (b + 1), :], in_=result[:])
 
-        for u in range(2):
-            for b in (0, 2):
-                weigh("ea", 0, b, b + 2, u, u + 1, 0)
-            for b in (0, 2):
-                weigh("eb", 0, b, b + 2, u, u + 1, 0)
-                add_aside(0, b, b + 2, u, u + 1)
-        for b in (0, 2):
-            weave(0, b)
-        for g in range(PASSES):
-            for b in range(BLOCKS):
-                given_pass(g, b, start=(g == 0))
-        weigh("ea", 1, 0, 1, 0, 2, 0)
-        weigh("ea", 1, 1, 2, 0, 2, 0)
-        quantise(0, 0, 2)
-        weigh("eb", 1, 0, 1, 0, 2, 0)
-        add_aside(1, 0, 1, 0, 2)
-        weave(1, 0)
-        quantise(0, 2, 4)
-        weigh("eb", 1, 1, 2, 0, 2, 0)
-        add_aside(1, 1, 2, 0, 2)
-        weave(1, 1)
-        for b in range(BLOCKS):
-            blended_pass(0, b)
-        weigh("ea", 1, 2, 3, 0, 2, 2)
-        weigh("eb", 1, 2, 3, 0, 2, 2)
-        add_aside(1, 2, 3, 0, 2)
-        quantise(1, 0, 1)
-        blended_pass(1, 0, stop=True)
-        weigh("ea", 1, 3, 4, 0, 2, 3)
-        quantise(1, 1, 2)
-        blended_pass(1, 1, stop=True)
-        weave(1, 2)
-        finish(0)
-        weigh("eb", 1, 3, 4, 0, 2, 3)
-        add_here(1, 3)
-        quantise(1, 2, 3)
-        blended_pass(1, 2, stop=True)
-        finish(1)
-        quantise(1, 3, 4)
-        blended_pass(1, 3, stop=True)
-        finish(2)
-        finish(3)
+        for i, (g, b) in enumerate(tiles[:-1]):
+            weigh_first(g, b)
+            weigh_second(g, b, 0, PACK)
+            join(nc.gpsimd, g, b, 0, PACK)
+            if i >= 2:
+                quantise(*tiles[i - 2])
+            weave(nc.scalar.copy, g, b)
+        for c in range(BLOCKS):
+            given_pass(0, c)
+        for c in range(BLOCKS):
+            blended_pass(0, c)
+        for c in range(BLOCKS):
+            given_pass(1, c)
+        blended_pass(1, 0)
+        weigh_first(1, 3)
+        weigh_second(1, 3, 0, 2)
+        weigh_second(1, 3, 2, 4)
+        quantise(1, 1)
+        blended_pass(1, 1)
+        join(nc.vector, 1, 3, 0, 2)
+        join(nc.vector, 1, 3, 2, 4)
+        finish(nc.scalar.copy, 0)
+        quantise(1, 2)
+        blended_pass(1, 2)
+        finish(nc.scalar.copy, 1)
+        weave(nc.vector.tensor_copy, 1, 3)
+        quantise(1, 3)
+        blended_pass(1, 3)
+        finish(nc.scalar.copy, 2)
+        finish(nc.vector.tensor_copy, 3)

@@ -64,18 +64,24 @@ def tile_mix_blended_weights_and_given_kernel(
             for b in range(b0, b1):
                 raw[name, g, b] = tile[:, :, P * (b - b0) : P * (b - b0 + 1)]
 
-        codes = {}
+        def load_last_rows(j0, j1):
+            tile = keep.tile([P, j1 - j0, P], F32, name="eb_last_%d" % j0)
+            rows = eb[512:1024, N - P : N].rearrange("(p j) n -> p j n", j=PACK)
+            nc.sync.dma_start(out=tile[:], in_=rows[:, j0:j1, :])
+            raw["eb", 1, 3, j0] = tile[:]
 
-        def load_fp8(name, words, g):
-            codes[name, g] = keep.tile([P, 512], U32, name="%s_codes_%d" % (name, g), align_bytes=64)
+        def load_fp8(name, words, n0, n1):
+            tile = keep.tile([P, PASSES, n1 - n0], U32, name=name, align_bytes=64)
             nc.sync.dma_start(
-                out=codes[name, g][:].bitcast(I32),
-                in_=words[g].rearrange("p n t -> p (n t)").bitcast(I32),
+                out=tile[:].bitcast(I32),
+                in_=words[:, :, n0:n1, :].rearrange("g p n t -> p g (n t)").bitcast(I32),
             )
+            return tile
 
-        def load_fp4(g):
-            codes["xq", g] = keep.tile([P, 2 * T], U8, name="xq_codes_%d" % g, align_bytes=64)
-            nc.sync.dma_start(out=codes["xq", g][:].bitcast(I32), in_=xq_words[g].bitcast(I32))
+        xq_codes = keep.tile([P, PASSES, 2 * T], U8, name="xq_codes", align_bytes=64)
+
+        def load_fp4():
+            nc.sync.dma_start(out=xq_codes[:].bitcast(I32), in_=xq_words.rearrange("g p c -> p g c").bitcast(I32))
 
         share = keep.tile([P, PACK], F32, name="share")
         nc.scalar.dma_start(out=share[:], in_=sh.rearrange("o (p c) -> p (o c)", p=P))
@@ -85,22 +91,25 @@ def tile_mix_blended_weights_and_given_kernel(
         load_rows("ea", 0, 2, 4)
         load_scales("wq", wq_scales)
         load_rows("eb", 0, 2, 4)
-        load_scales("xq", xq_scales)
-        load_fp4(0)
         load_rows("ea", 1, 0, 2)
+        load_scales("xq", xq_scales)
         load_rows("eb", 1, 0, 2)
-        load_fp8("wq", wq_words, 0)
-        load_xt_scales()
-        load_fp8("xt", xt_words, 0)
-        load_fp4(1)
-        load_rows("ea", 1, 2, 3)
+        load_fp4()
+        wq_codes = [load_fp8("wq_low", wq_words, 0, N // 2)]
+        load_rows("ea", 1, 2, 4)
         load_rows("eb", 1, 2, 3)
-        load_fp8("wq", wq_words, 1)
-        load_rows("ea", 1, 3, 4)
-        load_rows("eb", 1, 3, 4)
-        load_fp8("xt", xt_words, 1)
+        load_xt_scales()
+        xt_codes = load_fp8("xt_codes", xt_words, 0, T)
+        load_last_rows(0, 2)
+        load_last_rows(2, 4)
+        wq_codes.append(load_fp8("wq_high", wq_words, N // 2, N))
 
-        acc = [sums.tile([P, T], F32, name="acc_%d" % b) for b in range(BLOCKS)]
+        spans = {b: [(0, T)] for b in range(BLOCKS - 1)}
+        spans[BLOCKS - 1] = [(0, T // 2), (T // 2, T)]
+        acc = {}
+        for b in range(BLOCKS):
+            for t0, t1 in spans[b]:
+                acc[b, t0] = sums.tile([P, t1 - t0], F32, name="acc_%d_%d" % (b, t0))
         spread = sums.tile([P, N], F32, name="spread")
         for c in range(PACK):
             nc.tensor.transpose(spread[:, c:N:PACK], share[:, c : c + 1].to_broadcast([P, P]), ident[:])
@@ -129,12 +138,12 @@ def tile_mix_blended_weights_and_given_kernel(
                 op=MULT,
             )
 
-        def weigh_second(g, b, j0, j1):
+        def weigh_second(g, b, j0, j1, rows):
             nc.vector.scalar_tensor_tensor(
                 out=second[g, b][:, P * j0 : P * j1].rearrange("p (j n) -> p j n", j=j1 - j0),
                 in0=factor(b, j1 - j0),
                 scalar=1.0,
-                in1=raw["eb", g, b][:, j0:j1, :],
+                in1=rows,
                 op0=SUBTRACT,
                 op1=MULT,
             )
@@ -160,60 +169,69 @@ def tile_mix_blended_weights_and_given_kernel(
 
         def given_pass(g, b):
             cols = slice(P * b, P * (b + 1))
-            nc.tensor.matmul_mx(
-                out=acc[b][:],
-                lhsT=codes["wq", g][:, cols].bitcast(FP8X4),
-                lhsT_scale=planes["wq"][:, g, cols],
-                rhs=codes["xq", g][:].bitcast(FP4X4),
-                rhs_scale=planes["xq"][:, g, :],
-                start=(g == 0),
-                stop=False,
-            )
+            for t0, t1 in spans[b]:
+                step = T if t1 - t0 == T else P
+                for t in range(t0, t1, step):
+                    nc.tensor.matmul_mx(
+                        out=acc[b, t0][:, t - t0 : t - t0 + step],
+                        lhsT=wq_codes[b // 2][:, g, P * (b % 2) : P * (b % 2 + 1)].bitcast(FP8X4),
+                        lhsT_scale=planes["wq"][:, g, cols],
+                        rhs=xq_codes[:, g, 2 * t : 2 * (t + step)].bitcast(FP4X4),
+                        rhs_scale=planes["xq"][:, g, t : t + step],
+                        start=(g == 0 and b < 2),
+                        stop=False,
+                    )
 
         def blended_pass(g, b):
             cols = slice(P * b, P * (b + 1))
-            nc.tensor.matmul_mx(
-                out=acc[b][:],
-                lhsT=em_codes[g][:, cols].bitcast(FP8X4),
-                lhsT_scale=em_plane[g][:, cols],
-                rhs=codes["xt", g][:].bitcast(FP8X4),
-                rhs_scale=xt_plane[4 + 4 * g : P, :],
-                start=False,
-                stop=(g == PASSES - 1),
-            )
+            for t0, t1 in spans[b]:
+                nc.tensor.matmul_mx(
+                    out=acc[b, t0][:],
+                    lhsT=em_codes[g][:, cols].bitcast(FP8X4),
+                    lhsT_scale=em_plane[g][:, cols],
+                    rhs=xt_codes[:, g, t0:t1].bitcast(FP8X4),
+                    rhs_scale=xt_plane[4 + 4 * g : P, t0:t1],
+                    start=(g == 0 and b >= 2),
+                    stop=(g == PASSES - 1),
+                )
 
-        def finish(copy, b):
-            result = keep.tile([P, T], F32, name="result_%d" % b)
-            copy(out=result[:], in_=acc[b][:])
-            nc.sync.dma_start(out=out[P * b : P * (b + 1), :], in_=result[:])
+        def finish(copy, b, t0, t1):
+            result = keep.tile([P, t1 - t0], F32, name="result_%d_%d" % (b, t0))
+            copy(out=result[:], in_=acc[b, t0][:])
+            nc.sync.dma_start(out=out[P * b : P * (b + 1), t0:t1], in_=result[:])
 
         for i, (g, b) in enumerate(tiles[:-1]):
             weigh_first(g, b)
-            weigh_second(g, b, 0, PACK)
+            weigh_second(g, b, 0, PACK, raw["eb", g, b])
             join(nc.gpsimd, g, b, 0, PACK)
             if i >= 2:
                 quantise(*tiles[i - 2])
             weave(nc.scalar.copy, g, b)
-        for c in range(BLOCKS):
-            given_pass(0, c)
-        for c in range(BLOCKS):
-            blended_pass(0, c)
-        for c in range(BLOCKS):
-            given_pass(1, c)
-        blended_pass(1, 0)
         weigh_first(1, 3)
-        weigh_second(1, 3, 0, 2)
-        weigh_second(1, 3, 2, 4)
         quantise(1, 1)
-        blended_pass(1, 1)
-        join(nc.vector, 1, 3, 0, 2)
-        join(nc.vector, 1, 3, 2, 4)
-        finish(nc.scalar.copy, 0)
+        for j in (0, 2):
+            weigh_second(1, 3, j, j + 2, raw["eb", 1, 3, j])
+        for j in (0, 2):
+            join(nc.vector, 1, 3, j, j + 2)
         quantise(1, 2)
-        blended_pass(1, 2)
-        finish(nc.scalar.copy, 1)
         weave(nc.vector.tensor_copy, 1, 3)
         quantise(1, 3)
+
+        for g in range(PASSES):
+            for b in (0, 1):
+                given_pass(g, b)
+        blended_pass(0, 0)
+        blended_pass(1, 0)
+        for b in (1, 2, 3):
+            blended_pass(0, b)
+        blended_pass(1, 1)
+        given_pass(0, 2)
+        given_pass(1, 2)
+        given_pass(0, 3)
+        blended_pass(1, 2)
+        given_pass(1, 3)
         blended_pass(1, 3)
-        finish(nc.scalar.copy, 2)
-        finish(nc.vector.tensor_copy, 3)
+        for b in range(BLOCKS - 1):
+            finish(nc.scalar.copy, b, 0, T)
+        finish(nc.vector.tensor_copy, 3, 0, T // 2)
+        finish(nc.scalar.copy, 3, T // 2, T)

@@ -18,9 +18,13 @@ SUBTRACT = mybir.AluOpType.subtract
 
 P = 128
 PACK = 4
-PASSES = 2
+K_PASS = P * PACK
+PASSES = K // K_PASS
 BLOCKS = N // P
-WIDTH = PACK * P
+LAST = BLOCKS - 1
+QUADRANT = 32
+SCALE_ROWS = 4
+GPSIMD_TILES = 5
 
 
 def tile_mix_blended_weights_and_given_kernel(
@@ -35,81 +39,67 @@ def tile_mix_blended_weights_and_given_kernel(
         ident = keep.tile([P, P], F32, name="ident")
         make_identity(nc, ident[:])
 
-        planes = {}
-        for name in ("wq", "xq"):
-            planes[name] = keep.tile([P, PASSES, 512], U8, name=name + "_plane", align_bytes=64)
-            nc.vector.memset(planes[name][:].rearrange("p g n -> p (g n)").bitcast(I32), 0)
+        wq_plane = keep.tile([P, PASSES, N], U8, name="wq_plane", align_bytes=64)
+        xq_plane = keep.tile([P, PASSES, T], U8, name="xq_plane", align_bytes=64)
         xt_plane = keep.tile([P, T], U8, name="xt_plane", align_bytes=64)
+        for plane in (wq_plane, xq_plane):
+            nc.vector.memset(plane[:].rearrange("p g n -> p (g n)").bitcast(I32), 0)
         nc.vector.memset(xt_plane[:].bitcast(I32), 0)
 
-        def load_scales(name, scales):
-            rows = scales.rearrange("g (q r) n -> r q g n", r=4)
-            for r in range(4):
-                nc.sync.dma_start(out=planes[name][r:P:32, :, :].bitcast(I32), in_=rows[r].bitcast(I32))
+        def load_scales(queue, plane, scales):
+            rows = scales.rearrange("g (q r) n -> r q g n", r=SCALE_ROWS)
+            for r in range(SCALE_ROWS):
+                queue.dma_start(out=plane[r:P:QUADRANT, :, :].bitcast(I32), in_=rows[r].bitcast(I32))
 
         def load_xt_scales():
-            for q in range(4):
+            for q in range(P // QUADRANT):
+                lowest = QUADRANT * q + SCALE_ROWS
                 nc.sync.dma_start(
-                    out=xt_plane[32 * q + 4 : 32 * q + 12, :].bitcast(I32),
-                    in_=xt_scales[:, 4 * q : 4 * q + 4, :].bitcast(I32),
+                    out=xt_plane[lowest : lowest + PASSES * SCALE_ROWS, :].bitcast(I32),
+                    in_=xt_scales[:, SCALE_ROWS * q : SCALE_ROWS * (q + 1), :].bitcast(I32),
                 )
 
-        source = {"ea": ea, "eb": eb}
-        raw = {}
-
-        def load_rows(name, g, b0, b1):
-            tile = keep.tile([P, PACK, P * (b1 - b0)], F32, name="%s_%d_%d" % (name, g, b0))
-            rows = source[name][512 * g : 512 * (g + 1), P * b0 : P * b1]
-            nc.sync.dma_start(out=tile[:], in_=rows.rearrange("(p j) n -> p j n", j=PACK))
-            for b in range(b0, b1):
-                raw[name, g, b] = tile[:, :, P * (b - b0) : P * (b - b0 + 1)]
-
-        def load_last_rows(j0, j1):
-            tile = keep.tile([P, j1 - j0, P], F32, name="eb_last_%d" % j0)
-            rows = eb[512:1024, N - P : N].rearrange("(p j) n -> p j n", j=PACK)
+        def load_rows(matrix, name, g, b0, b1, j0=0, j1=PACK):
+            tile = keep.tile([P, j1 - j0, P * (b1 - b0)], F32, name="%s_%d_%d_%d" % (name, g, b0, j0))
+            rows = matrix[K_PASS * g : K_PASS * (g + 1), P * b0 : P * b1].rearrange("(p j) n -> p j n", j=PACK)
             nc.sync.dma_start(out=tile[:], in_=rows[:, j0:j1, :])
-            raw["eb", 1, 3, j0] = tile[:]
+            return {(g, b): tile[:, :, P * (b - b0) : P * (b - b0 + 1)] for b in range(b0, b1)}
 
-        def load_fp8(name, words, n0, n1):
-            tile = keep.tile([P, PASSES, n1 - n0], U32, name=name, align_bytes=64)
+        def load_words(name, words, c0, c1):
+            tile = keep.tile([P, PASSES, c1 - c0], U32, name=name, align_bytes=64)
             nc.sync.dma_start(
                 out=tile[:].bitcast(I32),
-                in_=words[:, :, n0:n1, :].rearrange("g p n t -> p g (n t)").bitcast(I32),
+                in_=words[:, :, c0:c1, :].rearrange("g p c j -> p g (c j)").bitcast(I32),
             )
             return tile
 
-        xq_codes = keep.tile([P, PASSES, 2 * T], U8, name="xq_codes", align_bytes=64)
-
-        def load_fp4():
-            nc.sync.dma_start(out=xq_codes[:].bitcast(I32), in_=xq_words.rearrange("g p c -> p g c").bitcast(I32))
-
         share = keep.tile([P, PACK], F32, name="share")
         nc.scalar.dma_start(out=share[:], in_=sh.rearrange("o (p c) -> p (o c)", p=P))
-        for b in range(2):
-            load_rows("ea", 0, b, b + 1)
-            load_rows("eb", 0, b, b + 1)
-        load_rows("ea", 0, 2, 4)
-        load_scales("wq", wq_scales)
-        load_rows("eb", 0, 2, 4)
-        load_rows("ea", 1, 0, 2)
-        load_scales("xq", xq_scales)
-        load_rows("eb", 1, 0, 2)
-        load_fp4()
-        wq_codes = [load_fp8("wq_low", wq_words, 0, N // 2)]
-        load_rows("ea", 1, 2, 4)
-        load_rows("eb", 1, 2, 3)
+        load_scales(nc.gpsimd, wq_plane, wq_scales)
+        ea_rows = {}
+        eb_rows = {}
+        for g, b0, b1 in ((0, 0, 1), (0, 1, 2), (0, 2, 4), (1, 0, 2)):
+            ea_rows.update(load_rows(ea, "ea", g, b0, b1))
+            eb_rows.update(load_rows(eb, "eb", g, b0, b1))
+        ea_rows.update(load_rows(ea, "ea", 1, 2, 4))
+        load_scales(nc.sync, xq_plane, xq_scales)
+        xq_codes = keep.tile([P, PASSES, 2 * T], U8, name="xq_codes", align_bytes=64)
+        nc.sync.dma_start(out=xq_codes[:].bitcast(I32), in_=xq_words.rearrange("g p c -> p g c").bitcast(I32))
+        wq_low = load_words("wq_low", wq_words, 0, N // 2)
+        eb_rows.update(load_rows(eb, "eb", 1, 2, 3))
         load_xt_scales()
-        xt_codes = load_fp8("xt_codes", xt_words, 0, T)
-        load_last_rows(0, 2)
-        load_last_rows(2, 4)
-        wq_codes.append(load_fp8("wq_high", wq_words, N // 2, N))
+        xt_codes = load_words("xt_codes", xt_words, 0, T)
+        halves = ((0, PACK // 2), (PACK // 2, PACK))
+        eb_last = [load_rows(eb, "eb", 1, LAST, BLOCKS, j0, j1)[1, LAST] for j0, j1 in halves]
+        wq_high = load_words("wq_high", wq_words, N // 2, N)
 
-        spans = {b: [(0, T)] for b in range(BLOCKS - 1)}
-        spans[BLOCKS - 1] = [(0, T // 2), (T // 2, T)]
+        spans = {b: [(0, T)] for b in range(LAST)}
+        spans[LAST] = [(0, T // 2), (T // 2, T)]
         acc = {}
         for b in range(BLOCKS):
             for t0, t1 in spans[b]:
                 acc[b, t0] = sums.tile([P, t1 - t0], F32, name="acc_%d_%d" % (b, t0))
+
         spread = sums.tile([P, N], F32, name="spread")
         for c in range(PACK):
             nc.tensor.transpose(spread[:, c:N:PACK], share[:, c : c + 1].to_broadcast([P, P]), ident[:])
@@ -117,81 +107,80 @@ def tile_mix_blended_weights_and_given_kernel(
         tiles = [(g, b) for g in range(PASSES) for b in range(BLOCKS)]
         first = {}
         second = {}
-        total = {}
-        grouped = {}
+        joined = {}
         for g, b in tiles:
-            first[g, b] = keep.tile([P, WIDTH], F32, name="first_%d_%d" % (g, b))
-            second[g, b] = keep.tile([P, WIDTH], F32, name="second_%d_%d" % (g, b))
-            total[g, b] = keep.tile([P, WIDTH], BF16, name="total_%d_%d" % (g, b))
-            grouped[g, b] = keep.tile([P, WIDTH], BF16, name="grouped_%d_%d" % (g, b), align_bytes=64)
+            first[g, b] = keep.tile([P, PACK * P], F32, name="first_%d_%d" % (g, b))
+            second[g, b] = keep.tile([P, PACK * P], F32, name="second_%d_%d" % (g, b))
+            joined[g, b] = keep.tile([P, PACK * P], BF16, name="joined_%d_%d" % (g, b))
+        grouped = [keep.tile([P, PACK * N], BF16, name="grouped_%d" % g, align_bytes=64) for g in range(PASSES)]
         em_codes = [keep.tile([P, N], U32, name="em_codes_%d" % g, align_bytes=64) for g in range(PASSES)]
         em_plane = [keep.tile([P, N], U8, name="em_plane_%d" % g, align_bytes=64) for g in range(PASSES)]
 
-        def factor(b, rows):
+        def shares(b, rows):
             return spread[:, P * b : P * (b + 1)].unsqueeze(1).to_broadcast([P, rows, P])
 
         def weigh_first(g, b):
             nc.vector.tensor_tensor(
                 out=first[g, b][:].rearrange("p (j n) -> p j n", j=PACK),
-                in0=raw["ea", g, b],
-                in1=factor(b, PACK),
+                in0=ea_rows[g, b],
+                in1=shares(b, PACK),
                 op=MULT,
             )
 
-        def weigh_second(g, b, j0, j1, rows):
+        def weigh_second(g, b, rows, j0=0, j1=PACK):
             nc.vector.scalar_tensor_tensor(
                 out=second[g, b][:, P * j0 : P * j1].rearrange("p (j n) -> p j n", j=j1 - j0),
-                in0=factor(b, j1 - j0),
+                in0=shares(b, j1 - j0),
                 scalar=1.0,
                 in1=rows,
                 op0=SUBTRACT,
                 op1=MULT,
             )
 
-        def join(engine, g, b, j0, j1):
+        def join(engine, g, b, j0=0, j1=PACK):
             cols = slice(P * j0, P * j1)
             engine.tensor_tensor(
-                out=total[g, b][:, cols], in0=first[g, b][:, cols], in1=second[g, b][:, cols], op=SUBTRACT
+                out=joined[g, b][:, cols], in0=first[g, b][:, cols], in1=second[g, b][:, cols], op=SUBTRACT
             )
 
         def weave(copy, g, b):
             copy(
-                out=grouped[g, b][:].rearrange("p (n j) -> p n j", j=PACK),
-                in_=total[g, b][:].rearrange("p (j n) -> p n j", j=PACK),
+                out=grouped[g][:, PACK * P * b : PACK * P * (b + 1)].rearrange("p (n j) -> p n j", j=PACK),
+                in_=joined[g, b][:].rearrange("p (j n) -> p n j", j=PACK),
             )
 
-        def quantise(g, b):
+        def quantise(g, b0, b1):
             nc.vector.quantize_mx(
-                out=em_codes[g][:, P * b : P * (b + 1)].bitcast(FP8X4),
-                scales=em_plane[g][:, P * b : P * (b + 1)],
-                in_=grouped[g, b][:],
+                out=em_codes[g][:, P * b0 : P * b1].bitcast(FP8X4),
+                scales=em_plane[g][:, P * b0 : P * b1],
+                in_=grouped[g][:, PACK * P * b0 : PACK * P * b1],
             )
 
-        def given_pass(g, b):
-            cols = slice(P * b, P * (b + 1))
+        def given_pass(g, b, start=False):
+            wq_codes = wq_low if b < BLOCKS // 2 else wq_high
+            c0 = P * (b % (BLOCKS // 2))
             for t0, t1 in spans[b]:
-                step = T if t1 - t0 == T else P
-                for t in range(t0, t1, step):
+                width = T if t1 - t0 == T else P
+                for t in range(t0, t1, width):
                     nc.tensor.matmul_mx(
-                        out=acc[b, t0][:, t - t0 : t - t0 + step],
-                        lhsT=wq_codes[b // 2][:, g, P * (b % 2) : P * (b % 2 + 1)].bitcast(FP8X4),
-                        lhsT_scale=planes["wq"][:, g, cols],
-                        rhs=xq_codes[:, g, 2 * t : 2 * (t + step)].bitcast(FP4X4),
-                        rhs_scale=planes["xq"][:, g, t : t + step],
-                        start=(g == 0 and b < 2),
+                        out=acc[b, t0][:, t - t0 : t - t0 + width],
+                        lhsT=wq_codes[:, g, c0 : c0 + P].bitcast(FP8X4),
+                        lhsT_scale=wq_plane[:, g, P * b : P * (b + 1)],
+                        rhs=xq_codes[:, g, 2 * t : 2 * (t + width)].bitcast(FP4X4),
+                        rhs_scale=xq_plane[:, g, t : t + width],
+                        start=start,
                         stop=False,
                     )
 
-        def blended_pass(g, b):
-            cols = slice(P * b, P * (b + 1))
+        def blended_pass(g, b, start=False):
             for t0, t1 in spans[b]:
                 nc.tensor.matmul_mx(
                     out=acc[b, t0][:],
-                    lhsT=em_codes[g][:, cols].bitcast(FP8X4),
-                    lhsT_scale=em_plane[g][:, cols],
+                    lhsT=em_codes[g][:, P * b : P * (b + 1)].bitcast(FP8X4),
+                    lhsT_scale=em_plane[g][:, P * b : P * (b + 1)],
                     rhs=xt_codes[:, g, t0:t1].bitcast(FP8X4),
-                    rhs_scale=xt_plane[4 + 4 * g : P, t0:t1],
-                    start=(g == 0 and b >= 2),
+                    rhs_scale=xt_plane[SCALE_ROWS * (g + 1) : P, t0:t1],
+                    start=start,
                     stop=(g == PASSES - 1),
                 )
 
@@ -200,38 +189,45 @@ def tile_mix_blended_weights_and_given_kernel(
             copy(out=result[:], in_=acc[b, t0][:])
             nc.sync.dma_start(out=out[P * b : P * (b + 1), t0:t1], in_=result[:])
 
-        for i, (g, b) in enumerate(tiles[:-1]):
+        for g, b in tiles[:GPSIMD_TILES]:
             weigh_first(g, b)
-            weigh_second(g, b, 0, PACK, raw["eb", g, b])
-            join(nc.gpsimd, g, b, 0, PACK)
-            if i >= 2:
-                quantise(*tiles[i - 2])
+            weigh_second(g, b, eb_rows[g, b])
+            join(nc.gpsimd, g, b)
             weave(nc.scalar.copy, g, b)
-        weigh_first(1, 3)
-        quantise(1, 1)
-        for j in (0, 2):
-            weigh_second(1, 3, j, j + 2, raw["eb", 1, 3, j])
-        for j in (0, 2):
-            join(nc.vector, 1, 3, j, j + 2)
-        quantise(1, 2)
-        weave(nc.vector.tensor_copy, 1, 3)
-        quantise(1, 3)
+
+        weigh_first(1, 1)
+        weigh_second(1, 1, eb_rows[1, 1])
+        weigh_first(1, 2)
+        weigh_first(1, LAST)
+        join(nc.vector, 1, 1)
+        weave(nc.scalar.copy, 1, 1)
+        quantise(0, 0, BLOCKS)
+        weigh_second(1, 2, eb_rows[1, 2])
+        quantise(1, 0, 2)
+        join(nc.vector, 1, 2)
+        weave(nc.scalar.copy, 1, 2)
+        for rows, (j0, j1) in zip(eb_last, halves):
+            weigh_second(1, LAST, rows, j0, j1)
+        for j0, j1 in halves:
+            join(nc.vector, 1, LAST, j0, j1)
+        quantise(1, 2, LAST)
+        weave(nc.vector.tensor_copy, 1, LAST)
+        quantise(1, LAST, BLOCKS)
 
         for g in range(PASSES):
             for b in (0, 1):
+                given_pass(g, b, start=(g == 0))
+        for b in (0, 1):
+            for g in range(PASSES):
+                blended_pass(g, b)
+        for b in (2, LAST):
+            blended_pass(0, b, start=True)
+        for b in (2, LAST):
+            for g in range(PASSES):
                 given_pass(g, b)
-        blended_pass(0, 0)
-        blended_pass(1, 0)
-        for b in (1, 2, 3):
-            blended_pass(0, b)
-        blended_pass(1, 1)
-        given_pass(0, 2)
-        given_pass(1, 2)
-        given_pass(0, 3)
-        blended_pass(1, 2)
-        given_pass(1, 3)
-        blended_pass(1, 3)
-        for b in range(BLOCKS - 1):
+            blended_pass(1, b)
+
+        for b in range(LAST):
             finish(nc.scalar.copy, b, 0, T)
-        finish(nc.vector.tensor_copy, 3, 0, T // 2)
-        finish(nc.scalar.copy, 3, T // 2, T)
+        for copy, (t0, t1) in zip((nc.vector.tensor_copy, nc.scalar.copy), spans[LAST]):
+            finish(copy, LAST, t0, t1)

from contextlib import ExitStack

import concourse.mybir as mybir
from concourse.masks import make_identity

K, L, T, N = 1024, 1024, 512, 512
FLOPS = 2 * N * T * (K + L)

F32 = mybir.dt.float32
BF16 = mybir.dt.bfloat16
I32 = mybir.dt.int32
U32 = mybir.dt.uint32
U8 = mybir.dt.uint8
FP8X4 = mybir.dt.float8_e4m3fn_x4
FP4X4 = mybir.dt.float4_e2m1fn_x4
MULT = mybir.AluOpType.mult
SUBTRACT = mybir.AluOpType.subtract

P = 128
PACK = 4
K_PASS = P * PACK
PASSES = K // K_PASS
BLOCKS = N // P
LAST = BLOCKS - 1
QUADRANT = 32
SCALE_ROWS = 4
GPSIMD_TILES = 5


def tile_mix_blended_weights_and_given_kernel(
    tc, xt_words, xt_scales, ea, eb, sh, xq_words, xq_scales, wq_words, wq_scales, out
):
    nc = tc.nc
    with ExitStack() as ctx:
        keep = ctx.enter_context(tc.tile_pool(name="keep", bufs=1))
        sums = ctx.enter_context(tc.psum_pool(name="sums", bufs=1))
        ctx.enter_context(tc.manual_schedule())

        ident = keep.tile([P, P], F32, name="ident")
        make_identity(nc, ident[:])

        wq_plane = keep.tile([P, PASSES, N], U8, name="wq_plane", align_bytes=64)
        xq_plane = keep.tile([P, PASSES, T], U8, name="xq_plane", align_bytes=64)
        xt_plane = keep.tile([P, T], U8, name="xt_plane", align_bytes=64)
        for plane in (wq_plane, xq_plane):
            nc.vector.memset(plane[:].rearrange("p g n -> p (g n)").bitcast(I32), 0)
        nc.vector.memset(xt_plane[:].bitcast(I32), 0)

        def load_scales(queue, plane, scales):
            rows = scales.rearrange("g (q r) n -> r q g n", r=SCALE_ROWS)
            for r in range(SCALE_ROWS):
                queue.dma_start(out=plane[r:P:QUADRANT, :, :].bitcast(I32), in_=rows[r].bitcast(I32))

        def load_xt_scales():
            for q in range(P // QUADRANT):
                lowest = QUADRANT * q + SCALE_ROWS
                nc.sync.dma_start(
                    out=xt_plane[lowest : lowest + PASSES * SCALE_ROWS, :].bitcast(I32),
                    in_=xt_scales[:, SCALE_ROWS * q : SCALE_ROWS * (q + 1), :].bitcast(I32),
                )

        def load_rows(matrix, name, g, b0, b1, j0=0, j1=PACK):
            tile = keep.tile([P, j1 - j0, P * (b1 - b0)], F32, name="%s_%d_%d_%d" % (name, g, b0, j0))
            rows = matrix[K_PASS * g : K_PASS * (g + 1), P * b0 : P * b1].rearrange("(p j) n -> p j n", j=PACK)
            nc.sync.dma_start(out=tile[:], in_=rows[:, j0:j1, :])
            return {(g, b): tile[:, :, P * (b - b0) : P * (b - b0 + 1)] for b in range(b0, b1)}

        def load_words(name, words, c0, c1):
            tile = keep.tile([P, PASSES, c1 - c0], U32, name=name, align_bytes=64)
            nc.sync.dma_start(
                out=tile[:].bitcast(I32),
                in_=words[:, :, c0:c1, :].rearrange("g p c j -> p g (c j)").bitcast(I32),
            )
            return tile

        share = keep.tile([P, PACK], F32, name="share")
        nc.scalar.dma_start(out=share[:], in_=sh.rearrange("o (p c) -> p (o c)", p=P))
        load_scales(nc.gpsimd, wq_plane, wq_scales)
        ea_rows = {}
        eb_rows = {}
        for g, b0, b1 in ((0, 0, 1), (0, 1, 2), (0, 2, 4), (1, 0, 2)):
            ea_rows.update(load_rows(ea, "ea", g, b0, b1))
            eb_rows.update(load_rows(eb, "eb", g, b0, b1))
        ea_rows.update(load_rows(ea, "ea", 1, 2, 4))
        load_scales(nc.sync, xq_plane, xq_scales)
        xq_codes = keep.tile([P, PASSES, 2 * T], U8, name="xq_codes", align_bytes=64)
        nc.sync.dma_start(out=xq_codes[:].bitcast(I32), in_=xq_words.rearrange("g p c -> p g c").bitcast(I32))
        wq_low = load_words("wq_low", wq_words, 0, N // 2)
        eb_rows.update(load_rows(eb, "eb", 1, 2, 3))
        load_xt_scales()
        xt_codes = load_words("xt_codes", xt_words, 0, T)
        halves = ((0, PACK // 2), (PACK // 2, PACK))
        eb_last = [load_rows(eb, "eb", 1, LAST, BLOCKS, j0, j1)[1, LAST] for j0, j1 in halves]
        wq_high = load_words("wq_high", wq_words, N // 2, N)

        spans = {b: [(0, T)] for b in range(LAST)}
        spans[LAST] = [(0, T // 2), (T // 2, T)]
        acc = {}
        for b in range(BLOCKS):
            for t0, t1 in spans[b]:
                acc[b, t0] = sums.tile([P, t1 - t0], F32, name="acc_%d_%d" % (b, t0))

        spread = sums.tile([P, N], F32, name="spread")
        for c in range(PACK):
            nc.tensor.transpose(spread[:, c:N:PACK], share[:, c : c + 1].to_broadcast([P, P]), ident[:])

        tiles = [(g, b) for g in range(PASSES) for b in range(BLOCKS)]
        first = {}
        second = {}
        joined = {}
        for g, b in tiles:
            first[g, b] = keep.tile([P, PACK * P], F32, name="first_%d_%d" % (g, b))
            second[g, b] = keep.tile([P, PACK * P], F32, name="second_%d_%d" % (g, b))
            joined[g, b] = keep.tile([P, PACK * P], BF16, name="joined_%d_%d" % (g, b))
        grouped = [keep.tile([P, PACK * N], BF16, name="grouped_%d" % g, align_bytes=64) for g in range(PASSES)]
        em_codes = [keep.tile([P, N], U32, name="em_codes_%d" % g, align_bytes=64) for g in range(PASSES)]
        em_plane = [keep.tile([P, N], U8, name="em_plane_%d" % g, align_bytes=64) for g in range(PASSES)]

        def shares(b, rows):
            return spread[:, P * b : P * (b + 1)].unsqueeze(1).to_broadcast([P, rows, P])

        def weigh_first(g, b):
            nc.vector.tensor_tensor(
                out=first[g, b][:].rearrange("p (j n) -> p j n", j=PACK),
                in0=ea_rows[g, b],
                in1=shares(b, PACK),
                op=MULT,
            )

        def weigh_second(g, b, rows, j0=0, j1=PACK):
            nc.vector.scalar_tensor_tensor(
                out=second[g, b][:, P * j0 : P * j1].rearrange("p (j n) -> p j n", j=j1 - j0),
                in0=shares(b, j1 - j0),
                scalar=1.0,
                in1=rows,
                op0=SUBTRACT,
                op1=MULT,
            )

        def join(engine, g, b, j0=0, j1=PACK):
            cols = slice(P * j0, P * j1)
            engine.tensor_tensor(
                out=joined[g, b][:, cols], in0=first[g, b][:, cols], in1=second[g, b][:, cols], op=SUBTRACT
            )

        def weave(copy, g, b):
            copy(
                out=grouped[g][:, PACK * P * b : PACK * P * (b + 1)].rearrange("p (n j) -> p n j", j=PACK),
                in_=joined[g, b][:].rearrange("p (j n) -> p n j", j=PACK),
            )

        def quantise(g, b0, b1):
            nc.vector.quantize_mx(
                out=em_codes[g][:, P * b0 : P * b1].bitcast(FP8X4),
                scales=em_plane[g][:, P * b0 : P * b1],
                in_=grouped[g][:, PACK * P * b0 : PACK * P * b1],
            )

        def given_pass(g, b, start=False):
            wq_codes = wq_low if b < BLOCKS // 2 else wq_high
            c0 = P * (b % (BLOCKS // 2))
            for t0, t1 in spans[b]:
                width = T if t1 - t0 == T else P
                for t in range(t0, t1, width):
                    nc.tensor.matmul_mx(
                        out=acc[b, t0][:, t - t0 : t - t0 + width],
                        lhsT=wq_codes[:, g, c0 : c0 + P].bitcast(FP8X4),
                        lhsT_scale=wq_plane[:, g, P * b : P * (b + 1)],
                        rhs=xq_codes[:, g, 2 * t : 2 * (t + width)].bitcast(FP4X4),
                        rhs_scale=xq_plane[:, g, t : t + width],
                        start=start,
                        stop=False,
                    )

        def blended_pass(g, b, start=False):
            for t0, t1 in spans[b]:
                nc.tensor.matmul_mx(
                    out=acc[b, t0][:],
                    lhsT=em_codes[g][:, P * b : P * (b + 1)].bitcast(FP8X4),
                    lhsT_scale=em_plane[g][:, P * b : P * (b + 1)],
                    rhs=xt_codes[:, g, t0:t1].bitcast(FP8X4),
                    rhs_scale=xt_plane[SCALE_ROWS * (g + 1) : P, t0:t1],
                    start=start,
                    stop=(g == PASSES - 1),
                )

        def finish(copy, b, t0, t1):
            result = keep.tile([P, t1 - t0], F32, name="result_%d_%d" % (b, t0))
            copy(out=result[:], in_=acc[b, t0][:])
            nc.sync.dma_start(out=out[P * b : P * (b + 1), t0:t1], in_=result[:])

        for g, b in tiles[:GPSIMD_TILES]:
            weigh_first(g, b)
            weigh_second(g, b, eb_rows[g, b])
            join(nc.gpsimd, g, b)
            weave(nc.scalar.copy, g, b)

        weigh_first(1, 1)
        weigh_second(1, 1, eb_rows[1, 1])
        weigh_first(1, 2)
        weigh_first(1, LAST)
        join(nc.vector, 1, 1)
        weave(nc.scalar.copy, 1, 1)
        quantise(0, 0, BLOCKS)
        weigh_second(1, 2, eb_rows[1, 2])
        quantise(1, 0, 2)
        join(nc.vector, 1, 2)
        weave(nc.scalar.copy, 1, 2)
        for rows, (j0, j1) in zip(eb_last, halves):
            weigh_second(1, LAST, rows, j0, j1)
        for j0, j1 in halves:
            join(nc.vector, 1, LAST, j0, j1)
        quantise(1, 2, LAST)
        weave(nc.vector.tensor_copy, 1, LAST)
        quantise(1, LAST, BLOCKS)

        for g in range(PASSES):
            for b in (0, 1):
                given_pass(g, b, start=(g == 0))
        for b in (0, 1):
            for g in range(PASSES):
                blended_pass(g, b)
        for b in (2, LAST):
            blended_pass(0, b, start=True)
        for b in (2, LAST):
            for g in range(PASSES):
                given_pass(g, b)
            blended_pass(1, b)

        for b in range(LAST):
            finish(nc.scalar.copy, b, 0, T)
        for copy, (t0, t1) in zip((nc.vector.tensor_copy, nc.scalar.copy), spans[LAST]):
            finish(copy, LAST, t0, t1)
